import numpy as np
import ml_dtypes


def mxq(x, axis, fmt="e4m3"):
    dtype, down = {"e4m3": (ml_dtypes.float8_e4m3fn, 7), "e5m2": (ml_dtypes.float8_e5m2, 14)}[fmt]
    v = np.moveaxis(np.asarray(x, np.float32).astype(ml_dtypes.bfloat16).astype(np.float64), axis, -1)
    blocks = v.reshape(v.shape[:-1] + (-1, 32))
    amax = np.abs(blocks).max(-1, keepdims=True)
    byte = np.maximum(np.where(amax > 0, np.frexp(amax)[1] - 1 + 127, 0) - down, 1)
    scale = np.exp2(byte - 127.0)
    codes = (blocks / scale).astype(np.float32).astype(dtype).astype(np.float64)
    return np.moveaxis((codes * scale).reshape(v.shape), -1, axis)


WIDE = False


def mx_kscale(k):
    if not WIDE:
        return np.ones(k)
    levels = np.array([10, -10, 5, -5, 0])
    if k % 512:
        return np.exp2(np.random.permutation(np.resize(levels, k // 32))).repeat(32)
    a = np.empty((k // 512, 16))
    for p in range(k // 512):
        a[p, :8] = np.random.permutation(np.resize(levels, 8))
        for g in range(8):
            far = levels[np.abs(levels - a[p, g]) >= 10]
            a[p, g + 8] = far[np.random.randint(len(far))]
    return np.exp2(a.ravel()).repeat(32)


def f64(x):
    return np.asarray(x).astype(np.float64)


def striped(idx):
    return np.tile(idx.reshape(-1, 16).T, (8, 1)).astype(np.uint16)


def unstriped(offs):
    return offs[:16].T.reshape(-1).astype(np.int64)


E2M1 = np.array([0.0, 0.5, 1.0, 1.5, 2.0, 3.0, 4.0, 6.0, -0.0, -0.5, -1.0, -1.5, -2.0, -3.0, -4.0, -6.0])


def pack_weight(w, fmt):
    k, n = w.shape
    w = f64(np.asarray(w, np.float32).astype(ml_dtypes.bfloat16)).reshape(k // 32, 32, n)
    amax = np.abs(w).max(1)
    if fmt == "e4m3":
        byte = np.frexp(amax)[1] - 1 + 127 - 7
    else:
        mant, ex = np.frexp(amax / 6.0)
        byte = np.where(mant > 0.5, ex, ex - 1) + 127
    byte = np.clip(np.where(amax > 0, byte, 1), 1, 254)
    scaled = (w * np.exp2(127.0 - byte)[:, None, :]).reshape(k, n).astype(np.float32)
    by_word = np.ascontiguousarray(scaled.reshape(k // 512, 128, 4, n).transpose(0, 1, 3, 2))
    if fmt == "e4m3":
        words = by_word.astype(ml_dtypes.float8_e4m3fn).view(np.uint8)
    else:
        c = by_word.astype(ml_dtypes.float4_e2m1fn).view(np.uint8) & 0xF
        words = (c[..., 0::2] | (c[..., 1::2] << 4)).reshape(k // 512, 128, 2 * n)
    return np.ascontiguousarray(words), np.ascontiguousarray(byte.astype(np.uint8).reshape(k // 512, 16, n))


def unpack_weight(words, scales, fmt):
    g, _, n = scales.shape
    words = np.ascontiguousarray(words).reshape(g, 128, n, -1)
    if fmt == "e4m3":
        vals = words.view(ml_dtypes.float8_e4m3fn).astype(np.float64)
    else:
        nib = np.empty((g, 128, n, 4), np.uint8)
        nib[..., 0::2] = words & 0xF
        nib[..., 1::2] = words >> 4
        vals = E2M1[nib]
    vals = vals * np.repeat(np.exp2(scales.astype(np.float64) - 127.0), 8, axis=1)[..., None]
    return vals.transpose(0, 1, 3, 2).reshape(g * 512, n)


def gelu(v):
    return 0.5 * v * (1.0 + np.tanh(np.sqrt(2.0 / np.pi) * (v + 0.044715 * v**3)))


def striped8(idx):
    return np.concatenate([v.reshape(-1, 16).T for v in idx]).astype(np.uint16)


def unstriped8(offs):
    return np.stack([offs[16 * g:16 * g + 16].T.reshape(-1) for g in range(8)]).astype(np.int64)


def runs(v, idx8):
    k = np.arange(v.shape[0])
    return v[k[:, None], idx8[k % 512 // 64]]


T, S, P, K, H, N = 2048, 1024, 512, 1024, 1536, 512

def setup_inputs():
    n = np.random.standard_normal
    s = mx_kscale(K)[:, None]
    u = mx_kscale(H)[:, None]
    d = {}
    d["tab_words"], d["tab_scales"] = pack_weight(n((K, T)) * s, "e4m3")
    d["offs"] = striped8(np.stack([np.random.permutation(T)[:S] for _ in range(8)]))
    d["w1"] = (2.0 * n((K, H)) / K ** 0.5 / s).astype(np.float32)
    d["gain"] = (np.exp(0.3 * n(H)) * u[:, 0]).astype(np.float32)
    d["pos1"] = striped(np.random.permutation(S)[:P])
    d["pos2"] = striped(np.random.permutation(S)[:P])
    d["w4_words"], d["w4_scales"] = pack_weight(n((H, N)) / H ** 0.5 / u, "e2m1")
    d["target"] = (0.8 * n((N, P))).astype(np.float32)
    return d

def reference(tab_words, tab_scales, offs, w1, gain, pos1, pos2, w4_words, w4_scales, target):
    v = runs(unpack_weight(tab_words, tab_scales, "e4m3"), unstriped8(offs))
    x = mxq(f64(w1), 0, "e4m3").T @ v
    h = f64(gain)[:, None] / (1.0 + np.abs(x))
    h1 = h[:, unstriped(pos1)]
    h2 = h[:, unstriped(pos2)]
    z = np.maximum(h1, h2) + h1
    w4 = unpack_weight(w4_words, w4_scales, "e2m1")
    y = w4.T @ mxq(z, 0, "e4m3")
    return np.square(y - f64(target))

@@ -1,0 +1,262 @@
+from contextlib import ExitStack
+
+import concourse.mybir as mybir
+
+T, S, NP, K, H, N = 2048, 1024, 512, 1024, 1536, 512
+FLOPS = 2 * K * H * S + 2 * H * N * NP
+
+F32 = mybir.dt.float32
+BF16 = mybir.dt.bfloat16
+I32 = mybir.dt.int32
+U32 = mybir.dt.uint32
+U16 = mybir.dt.uint16
+U8 = mybir.dt.uint8
+FP8X4 = mybir.dt.float8_e4m3fn_x4
+FP4X4 = mybir.dt.float4_e2m1fn_x4
+ALU = mybir.AluOpType
+ACT = mybir.ActivationFunctionType
+
+P = 128
+PACK = 4
+PASS = P * PACK
+KP = K // PASS
+HP = H // PASS
+BANK = 512
+HALF = NP // 2
+
+
+def tile_list_shot_deviation_scores_kernel(
+    tc, tab_words, tab_scales, offs, w1, gain, pos1, pos2, w4_words, w4_scales, target, out
+):
+    nc = tc.nc
+    with ExitStack() as ctx:
+        lists = ctx.enter_context(tc.tile_pool(name="lists", bufs=1))
+        keep = ctx.enter_context(tc.tile_pool(name="keep", bufs=1))
+        stage = ctx.enter_context(tc.tile_pool(name="stage", bufs=4))
+        work = ctx.enter_context(tc.tile_pool(name="work", bufs=2))
+        psum = ctx.enter_context(tc.psum_pool(name="psum", bufs=1))
+
+        offs_t = lists.tile([P, S // 16], U16, name="offs_t")
+        pos1_t = lists.tile([P, NP // 16], U16, name="pos1_t")
+        pos2_t = lists.tile([P, NP // 16], U16, name="pos2_t")
+
+        scale_win = keep.tile([P, T], U8, name="scale_win", align_bytes=64)
+        nc.vector.memset(scale_win[:].bitcast(I32), 0)
+
+        def staged(shape, dtype, name):
+            return stage.tile(shape, dtype, name=name, tag="staged", align_bytes=64)
+
+        word_win = {}
+
+        def load_words(a):
+            word_win[a] = staged([P, T], U32, f"word_win{a}")
+            nc.sync.dma_start(
+                out=word_win[a][:].bitcast(I32),
+                in_=tab_words[a].rearrange("p t i -> p (t i)").bitcast(I32),
+            )
+
+        raw = {}
+
+        def load_w1(b, a):
+            raw[b, a] = staged([P, PACK, PASS], F32, f"raw{b}{a}")
+            rows = w1[a * PASS : (a + 1) * PASS, b * PASS : (b + 1) * PASS]
+            nc.sync.dma_start(out=raw[b, a][:], in_=rows.rearrange("(p j) c -> p j c", j=PACK))
+
+        nc.sync.dma_start(offs_t[:], offs)
+        nc.sync.dma_start(pos1_t[:], pos1)
+        nc.sync.dma_start(pos2_t[:], pos2)
+        gain_t = keep.tile([P, HP, PACK], F32, name="gain_t")
+        nc.sync.dma_start(out=gain_t[:], in_=gain.rearrange("(b p t) -> p b t", p=P, t=PACK))
+        for a in range(KP):
+            load_w1(0, a)
+            load_words(a)
+        for a in range(KP):
+            for e in range(2):
+                nc.scalar.dma_start(
+                    out=scale_win[4 * a + e : P : 16, :].bitcast(I32),
+                    in_=tab_scales[a, e:16:2, :].bitcast(I32),
+                )
+
+        scale_pick = keep.tile([P, S], U8, name="scale_pick", align_bytes=64)
+        nc.vector.tensor_copy(scale_pick[:], scale_win[:].indirect(offs_t[:]))
+        tab_plane = keep.tile([P, S], U8, name="tab_plane", align_bytes=64)
+        nc.vector.tensor_copy(tab_plane[:].bitcast(I32), scale_pick[:].bitcast(I32))
+        for a, queue in enumerate((nc.scalar, nc.gpsimd)):
+            for e in range(2):
+                queue.dma_start(
+                    out=tab_plane[4 * a + 2 + e : P : 32, :].bitcast(I32),
+                    in_=scale_pick[16 + 4 * a + e : P : 32, :].bitcast(I32),
+                )
+
+        word_pick = {}
+
+        def gather_words(a):
+            for c in range(S // BANK):
+                tile = keep.tile([P, BANK], U32, name=f"word_pick{a}{c}", align_bytes=64)
+                cols = slice(c * BANK // 16, (c + 1) * BANK // 16)
+                nc.vector.tensor_copy(tile[:], word_win[a][:].indirect(offs_t[:, cols]))
+                word_pick[a, c] = tile
+
+        grouped = {}
+        w1_codes = {}
+        w1_plane = {}
+
+        def round_w1(b, a, copy):
+            grouped[b, a] = work.tile([P, PACK, P, PACK], BF16, name="w1_grouped", align_bytes=64)
+            dst = grouped[b, a][:].rearrange("p t m j -> p m j t")
+            src = raw[b, a][:].rearrange("p j (m t) -> p m j t", t=PACK)
+            copy(dst, src)
+
+        def quantise_w1(b, a):
+            codes = keep.tile([P, PASS], U32, name=f"w1_codes{b}{a}", align_bytes=64)
+            plane = keep.tile([P, PASS], U8, name=f"w1_plane{b}{a}", align_bytes=64)
+            nc.vector.quantize_mx(
+                out=codes[:].bitcast(FP8X4),
+                scales=plane[:],
+                in_=grouped[b, a][:].rearrange("p t m j -> p (t m j)"),
+            )
+            w1_codes[b, a] = codes
+            w1_plane[b, a] = plane
+
+        round_w1(0, 0, nc.scalar.copy)
+        gather_words(0)
+        quantise_w1(0, 0)
+        round_w1(0, 1, nc.scalar.copy)
+        quantise_w1(0, 1)
+        gather_words(1)
+        for b in range(1, HP):
+            for a in range(KP):
+                load_w1(b, a)
+
+        gain2_t = keep.tile([P, HP, PACK], F32, name="gain2_t")
+        nc.vector.tensor_scalar(gain2_t[:], gain_t[:], 2.0, None, ALU.mult)
+
+        acc = {(h, u): psum.tile([P, 2, HALF], F32, name=f"acc{h}{u}") for h in range(2) for u in range(2)}
+
+        def closeness(b, t):
+            banks = []
+            for c in range(S // BANK):
+                bank = psum.tile([P, BANK], F32, name="x_bank", bufs=4)
+                for a in range(KP):
+                    nc.tensor.matmul_mx(
+                        out=bank[:],
+                        lhsT=w1_codes[b, a][:, t * P : (t + 1) * P].bitcast(FP8X4),
+                        lhsT_scale=w1_plane[b, a][:, t * P : (t + 1) * P],
+                        rhs=word_pick[a, c][:].bitcast(FP8X4),
+                        rhs_scale=tab_plane[4 * a : P, c * BANK : (c + 1) * BANK],
+                        start=(a == 0),
+                        stop=(a == KP - 1),
+                    )
+                banks.append(bank)
+            mag = work.tile([P, S], F32, name="mag")
+            root = work.tile([P, S], F32, name="root")
+            close = work.tile([P, S], F32, name="close", bufs=3)
+            halves = [slice(c * BANK, (c + 1) * BANK) for c in range(S // BANK)]
+            for c, cols in enumerate(halves):
+                nc.scalar.activation(out=mag[:, cols], in_=banks[c][:], func=ACT.Abs)
+            for cols in halves:
+                nc.scalar.activation(out=root[:, cols], in_=mag[:, cols], func=ACT.Abs_reciprocal_sqrt, bias=1.0)
+            for cols in halves:
+                nc.scalar.activation(out=close[:, cols], in_=root[:, cols], func=ACT.Square)
+            return close
+
+        def pair_up(b, t, close, z_rows):
+            first = work.tile([P, NP], F32, name="first")
+            diff = work.tile([P, NP], F32, name="diff")
+            lift = work.tile([P, NP], F32, name="lift")
+            halves = [
+                (slice(h * HALF, (h + 1) * HALF), slice(h * HALF // 16, (h + 1) * HALF // 16)) for h in range(2)
+            ]
+            for cols, ent in halves:
+                nc.vector.tensor_copy(first[:, cols], close[:].indirect(pos1_t[:, ent]))
+            for cols, ent in halves:
+                nc.vector.tensor_tensor(diff[:, cols], close[:].indirect(pos2_t[:, ent]), first[:, cols], ALU.subtract)
+            for cols, ent in halves:
+                nc.vector.tensor_scalar(lift[:, cols], diff[:, cols], gain_t[:, b, t : t + 1], 0.0, ALU.mult, ALU.max)
+            for cols, ent in halves:
+                nc.vector.scalar_tensor_tensor(
+                    z_rows[:, t, cols], first[:, cols], gain2_t[:, b, t : t + 1], lift[:, cols], ALU.mult, ALU.add
+                )
+
+        def multiply_w4(b, h, codes, plane):
+            for i in range(N // P):
+                nc.tensor.matmul_mx(
+                    out=acc[h, i // 2][:, i % 2, :],
+                    lhsT=w4_codes[:, b, 2 * i * P : 2 * (i + 1) * P].bitcast(FP4X4),
+                    lhsT_scale=w4_plane[:, b, i * P : (i + 1) * P],
+                    rhs=codes.bitcast(FP8X4),
+                    rhs_scale=plane,
+                    start=(b == 0 and i % 2 == 0),
+                    stop=(b == HP - 1 and i % 2 == 1),
+                )
+
+        def group_z(z_rows, cols, copy):
+            width = cols.stop - cols.start
+            z_grouped = work.tile([P, width, PACK], BF16, name="z_grouped", align_bytes=64)
+            copy(
+                z_grouped[:].rearrange("p (c i) t -> p c t i", i=4),
+                z_rows[:, :, cols].rearrange("p t (c i) -> p c t i", i=4),
+            )
+            return z_grouped
+
+        def quantise_z(z_grouped):
+            width = z_grouped.shape[1]
+            z_codes = work.tile([P, width], U32, name="z_codes", align_bytes=64)
+            z_plane = work.tile([P, width], U8, name="z_plane", align_bytes=64)
+            nc.vector.quantize_mx(
+                out=z_codes[:].bitcast(FP8X4),
+                scales=z_plane[:],
+                in_=z_grouped[:].rearrange("p m t -> p (m t)"),
+            )
+            return z_codes, z_plane
+
+        pair_halves = [slice(h * HALF, (h + 1) * HALF) for h in range(2)]
+
+        for a in range(KP):
+            round_w1(1, a, nc.vector.tensor_copy)
+            quantise_w1(1, a)
+
+        w4_codes = staged([P, HP, 2 * N], U8, "w4_codes")
+        nc.sync.dma_start(
+            out=w4_codes[:].bitcast(I32), in_=w4_words.rearrange("a p c -> p a c").bitcast(I32)
+        )
+        w4_plane = staged([P, HP, N], U8, "w4_plane")
+        nc.gpsimd.memset(w4_plane[:].bitcast(I32), 0)
+        for q in range(4):
+            nc.sync.dma_start(
+                out=w4_plane[32 * q : 32 * q + 4].bitcast(I32),
+                in_=w4_scales[:, 4 * q : 4 * q + 4, :].rearrange("a q c -> q a c").bitcast(I32),
+            )
+
+        z_rows = {}
+        for b in range(HP):
+            z_rows[b] = work.tile([P, PACK, NP], BF16, name="z_rows")
+            for t in range(PACK):
+                close = closeness(b, t)
+                pair_up(b, t, close, z_rows[b])
+                if b == 1 and t < KP:
+                    round_w1(2, t, nc.scalar.copy)
+                    quantise_w1(2, t)
+                if b > 0 and t == 1:
+                    codes, plane = quantise_z(group_z(z_rows[b - 1], slice(0, NP), nc.scalar.copy))
+                    for h, cols in enumerate(pair_halves):
+                        multiply_w4(b - 1, h, codes[:, cols], plane[:, cols])
+        last = [
+            group_z(z_rows[HP - 1], cols, copy)
+            for cols, copy in zip(pair_halves, (nc.scalar.copy, nc.vector.tensor_copy))
+        ]
+        for h in range(2):
+            codes, plane = quantise_z(last[h])
+            multiply_w4(HP - 1, h, codes[:], plane[:])
+
+        target_t = staged([P, N // P, NP], F32, "target_t")
+        nc.sync.dma_start(out=target_t[:], in_=target.rearrange("(i p) m -> p i m", p=P))
+
+        out_rows = out.rearrange("(i p) m -> p i m", p=P)
+        for h, cols in enumerate(pair_halves):
+            for u in range(2):
+                dev = work.tile([P, 2, HALF], F32, name="dev", bufs=4)
+                nc.vector.tensor_tensor(dev[:], acc[h, u][:], target_t[:, 2 * u : 2 * u + 2, cols], ALU.subtract)
+                res = work.tile([P, 2, HALF], F32, name="res", bufs=4)
+                nc.scalar.activation(out=res[:], in_=dev[:], func=ACT.Square)
+                nc.sync.dma_start(out=out_rows[:, 2 * u : 2 * u + 2, cols], in_=res[:])

@@ -81,7 +81,7 @@ def tile_list_shot_deviation_scores_kernel(
         nc.vector.tensor_copy(scale_pick[:], scale_win[:].indirect(offs_t[:]))
         tab_plane = keep.tile([P, S], U8, name="tab_plane", align_bytes=64)
         nc.vector.tensor_copy(tab_plane[:].bitcast(I32), scale_pick[:].bitcast(I32))
-        for a, queue in enumerate((nc.scalar, nc.gpsimd)):
+        for a, queue in enumerate((nc.sync, nc.gpsimd)):
             for e in range(2):
                 queue.dma_start(
                     out=tab_plane[4 * a + 2 + e : P : 32, :].bitcast(I32),
@@ -128,9 +128,6 @@ def tile_list_shot_deviation_scores_kernel(
             for a in range(KP):
                 load_w1(b, a)
 
-        gain2_t = keep.tile([P, HP, PACK], F32, name="gain2_t")
-        nc.vector.tensor_scalar(gain2_t[:], gain_t[:], 2.0, None, ALU.mult)
-
         acc = {(h, u): psum.tile([P, 2, HALF], F32, name=f"acc{h}{u}") for h in range(2) for u in range(2)}
 
         def closeness(b, t):
@@ -160,22 +157,20 @@ def tile_list_shot_deviation_scores_kernel(
                 nc.scalar.activation(out=close[:, cols], in_=root[:, cols], func=ACT.Square)
             return close
 
-        def pair_up(b, t, close, z_rows):
+        pair_halves = [slice(h * HALF, (h + 1) * HALF) for h in range(2)]
+
+        def pair_up(b, t, close, first_h, larger):
             first = work.tile([P, NP], F32, name="first")
-            diff = work.tile([P, NP], F32, name="diff")
-            lift = work.tile([P, NP], F32, name="lift")
-            halves = [
-                (slice(h * HALF, (h + 1) * HALF), slice(h * HALF // 16, (h + 1) * HALF // 16)) for h in range(2)
-            ]
-            for cols, ent in halves:
-                nc.vector.tensor_copy(first[:, cols], close[:].indirect(pos1_t[:, ent]))
-            for cols, ent in halves:
-                nc.vector.tensor_tensor(diff[:, cols], close[:].indirect(pos2_t[:, ent]), first[:, cols], ALU.subtract)
-            for cols, ent in halves:
-                nc.vector.tensor_scalar(lift[:, cols], diff[:, cols], gain_t[:, b, t : t + 1], 0.0, ALU.mult, ALU.max)
-            for cols, ent in halves:
+            second = work.tile([P, NP], F32, name="second")
+            row_gain = gain_t[:, b, t : t + 1]
+            nc.vector.tensor_copy(first[:], close[:].indirect(pos1_t[:]))
+            nc.gpsimd.tensor_scalar(first_h[:, t, :], first[:], row_gain, 0.0, ALU.mult, ALU.add)
+            for cols in pair_halves:
+                entries = slice(cols.start // 16, cols.stop // 16)
+                nc.vector.tensor_copy(second[:, cols], close[:].indirect(pos2_t[:, entries]))
+            for cols in pair_halves:
                 nc.vector.scalar_tensor_tensor(
-                    z_rows[:, t, cols], first[:, cols], gain2_t[:, b, t : t + 1], lift[:, cols], ALU.mult, ALU.add
+                    larger[:, t, cols], second[:, cols], row_gain, first_h[:, t, cols], ALU.mult, ALU.max
                 )
 
         def multiply_w4(b, h, codes, plane):
@@ -190,27 +185,26 @@ def tile_list_shot_deviation_scores_kernel(
                     stop=(b == HP - 1 and i % 2 == 1),
                 )
 
-        def group_z(z_rows, cols, copy):
-            width = cols.stop - cols.start
-            z_grouped = work.tile([P, width, PACK], BF16, name="z_grouped", align_bytes=64)
-            copy(
-                z_grouped[:].rearrange("p (c i) t -> p c t i", i=4),
-                z_rows[:, :, cols].rearrange("p t (c i) -> p c t i", i=4),
-            )
-            return z_grouped
-
-        def quantise_z(z_grouped):
-            width = z_grouped.shape[1]
-            z_codes = work.tile([P, width], U32, name="z_codes", align_bytes=64)
-            z_plane = work.tile([P, width], U8, name="z_plane", align_bytes=64)
-            nc.vector.quantize_mx(
-                out=z_codes[:].bitcast(FP8X4),
-                scales=z_plane[:],
-                in_=z_grouped[:].rearrange("p m t -> p (m t)"),
-            )
-            return z_codes, z_plane
-
-        pair_halves = [slice(h * HALF, (h + 1) * HALF) for h in range(2)]
+        def second_stage(b, first_h, larger):
+            z_grouped = []
+            for cols in pair_halves:
+                tile = work.tile([P, HALF, PACK], BF16, name="z_grouped", align_bytes=64)
+                nc.vector.tensor_tensor(
+                    tile[:].rearrange("p (c i) t -> p c t i", i=4),
+                    larger[:, :, cols].rearrange("p t (c i) -> p c t i", i=4),
+                    first_h[:, :, cols].rearrange("p t (c i) -> p c t i", i=4),
+                    ALU.add,
+                )
+                z_grouped.append(tile)
+            for h in range(2):
+                z_codes = work.tile([P, HALF], U32, name="z_codes", align_bytes=64)
+                z_plane = work.tile([P, HALF], U8, name="z_plane", align_bytes=64)
+                nc.vector.quantize_mx(
+                    out=z_codes[:].bitcast(FP8X4),
+                    scales=z_plane[:],
+                    in_=z_grouped[h][:].rearrange("p m t -> p (m t)"),
+                )
+                multiply_w4(b, h, z_codes[:], z_plane[:])
 
         for a in range(KP):
             round_w1(1, a, nc.vector.tensor_copy)
@@ -228,26 +222,16 @@ def tile_list_shot_deviation_scores_kernel(
                 in_=w4_scales[:, 4 * q : 4 * q + 4, :].rearrange("a q c -> q a c").bitcast(I32),
             )
 
-        z_rows = {}
         for b in range(HP):
-            z_rows[b] = work.tile([P, PACK, NP], BF16, name="z_rows")
+            first_h = work.tile([P, PACK, NP], F32, name="first_h")
+            larger = work.tile([P, PACK, NP], F32, name="larger")
             for t in range(PACK):
                 close = closeness(b, t)
-                pair_up(b, t, close, z_rows[b])
+                pair_up(b, t, close, first_h, larger)
                 if b == 1 and t < KP:
                     round_w1(2, t, nc.scalar.copy)
                     quantise_w1(2, t)
-                if b > 0 and t == 1:
-                    codes, plane = quantise_z(group_z(z_rows[b - 1], slice(0, NP), nc.scalar.copy))
-                    for h, cols in enumerate(pair_halves):
-                        multiply_w4(b - 1, h, codes[:, cols], plane[:, cols])
-        last = [
-            group_z(z_rows[HP - 1], cols, copy)
-            for cols, copy in zip(pair_halves, (nc.scalar.copy, nc.vector.tensor_copy))
-        ]
-        for h in range(2):
-            codes, plane = quantise_z(last[h])
-            multiply_w4(HP - 1, h, codes[:], plane[:])
+            second_stage(b, first_h, larger)
 
         target_t = staged([P, N // P, NP], F32, "target_t")
         nc.sync.dma_start(out=target_t[:], in_=target.rearrange("(i p) m -> p i m", p=P))

@@ -41,7 +41,7 @@ def tile_list_shot_deviation_scores_kernel(
         pos2_t = lists.tile([P, NP // 16], U16, name="pos2_t")
 
         scale_win = keep.tile([P, T], U8, name="scale_win", align_bytes=64)
-        nc.vector.memset(scale_win[:].bitcast(I32), 0)
+        nc.gpsimd.memset(scale_win[:].bitcast(I32), 0)
 
         def staged(shape, dtype, name):
             return stage.tile(shape, dtype, name=name, tag="staged", align_bytes=64)
@@ -63,27 +63,28 @@ def tile_list_shot_deviation_scores_kernel(
             nc.sync.dma_start(out=raw[b, a][:], in_=rows.rearrange("(p j) c -> p j c", j=PACK))
 
         nc.sync.dma_start(offs_t[:], offs)
-        nc.sync.dma_start(pos1_t[:], pos1)
-        nc.sync.dma_start(pos2_t[:], pos2)
-        gain_t = keep.tile([P, HP, PACK], F32, name="gain_t")
-        nc.sync.dma_start(out=gain_t[:], in_=gain.rearrange("(b p t) -> p b t", p=P, t=PACK))
-        for a in range(KP):
-            load_w1(0, a)
-            load_words(a)
+        load_w1(0, 0)
         for a in range(KP):
             for e in range(2):
-                nc.scalar.dma_start(
+                nc.sync.dma_start(
                     out=scale_win[4 * a + e : P : 16, :].bitcast(I32),
                     in_=tab_scales[a, e:16:2, :].bitcast(I32),
                 )
+        load_words(0)
+        load_w1(0, 1)
+        load_words(1)
+        nc.sync.dma_start(pos1_t[:], pos1)
+        nc.sync.dma_start(pos2_t[:], pos2)
+        gain_t = keep.tile([P, HP, PACK], F32, name="gain_t")
+        nc.gpsimd.dma_start(out=gain_t[:], in_=gain.rearrange("(b p t) -> p b t", p=P, t=PACK))
 
         scale_pick = keep.tile([P, S], U8, name="scale_pick", align_bytes=64)
         nc.vector.tensor_copy(scale_pick[:], scale_win[:].indirect(offs_t[:]))
         tab_plane = keep.tile([P, S], U8, name="tab_plane", align_bytes=64)
         nc.vector.tensor_copy(tab_plane[:].bitcast(I32), scale_pick[:].bitcast(I32))
-        for a, queue in enumerate((nc.sync, nc.gpsimd)):
+        for a in range(KP):
             for e in range(2):
-                queue.dma_start(
+                nc.sync.dma_start(
                     out=tab_plane[4 * a + 2 + e : P : 32, :].bitcast(I32),
                     in_=scale_pick[16 + 4 * a + e : P : 32, :].bitcast(I32),
                 )
@@ -108,22 +109,18 @@ def tile_list_shot_deviation_scores_kernel(
             copy(dst, src)
 
         def quantise_w1(b, a):
-            codes = keep.tile([P, PASS], U32, name=f"w1_codes{b}{a}", align_bytes=64)
-            plane = keep.tile([P, PASS], U8, name=f"w1_plane{b}{a}", align_bytes=64)
+            w1_codes[b, a] = keep.tile([P, PASS], U32, name=f"w1_codes{b}{a}", align_bytes=64)
+            w1_plane[b, a] = keep.tile([P, PASS], U8, name=f"w1_plane{b}{a}", align_bytes=64)
             nc.vector.quantize_mx(
-                out=codes[:].bitcast(FP8X4),
-                scales=plane[:],
+                out=w1_codes[b, a][:].bitcast(FP8X4),
+                scales=w1_plane[b, a][:],
                 in_=grouped[b, a][:].rearrange("p t m j -> p (t m j)"),
             )
-            w1_codes[b, a] = codes
-            w1_plane[b, a] = plane
 
-        round_w1(0, 0, nc.scalar.copy)
-        gather_words(0)
-        quantise_w1(0, 0)
-        round_w1(0, 1, nc.scalar.copy)
-        quantise_w1(0, 1)
-        gather_words(1)
+        for a in range(KP):
+            round_w1(0, a, nc.scalar.copy)
+            gather_words(a)
+            quantise_w1(0, a)
         for b in range(1, HP):
             for a in range(KP):
                 load_w1(b, a)
@@ -209,6 +206,8 @@ def tile_list_shot_deviation_scores_kernel(
         for a in range(KP):
             round_w1(1, a, nc.vector.tensor_copy)
             quantise_w1(1, a)
+        round_w1(2, 0, nc.vector.tensor_copy)
+        quantise_w1(2, 0)
 
         w4_codes = staged([P, HP, 2 * N], U8, "w4_codes")
         nc.sync.dma_start(
@@ -228,19 +227,21 @@ def tile_list_shot_deviation_scores_kernel(
             for t in range(PACK):
                 close = closeness(b, t)
                 pair_up(b, t, close, first_h, larger)
-                if b == 1 and t < KP:
-                    round_w1(2, t, nc.scalar.copy)
-                    quantise_w1(2, t)
+                if (b, t) == (1, 0):
+                    round_w1(2, 1, nc.scalar.copy)
+                    quantise_w1(2, 1)
             second_stage(b, first_h, larger)
 
         target_t = staged([P, N // P, NP], F32, "target_t")
         nc.sync.dma_start(out=target_t[:], in_=target.rearrange("(i p) m -> p i m", p=P))
 
         out_rows = out.rearrange("(i p) m -> p i m", p=P)
-        for h, cols in enumerate(pair_halves):
-            for u in range(2):
-                dev = work.tile([P, 2, HALF], F32, name="dev", bufs=4)
-                nc.vector.tensor_tensor(dev[:], acc[h, u][:], target_t[:, 2 * u : 2 * u + 2, cols], ALU.subtract)
-                res = work.tile([P, 2, HALF], F32, name="res", bufs=4)
-                nc.scalar.activation(out=res[:], in_=dev[:], func=ACT.Square)
-                nc.sync.dma_start(out=out_rows[:, 2 * u : 2 * u + 2, cols], in_=res[:])
+        pieces = [(0, 0, 2), (0, 2, 4), (1, 0, 2), (1, 2, 3), (1, 3, 4)]
+        for h, lo, hi in pieces:
+            cols = pair_halves[h]
+            dev = work.tile([P, hi - lo, HALF], F32, name="dev", bufs=len(pieces))
+            sums = acc[h, lo // 2][:, lo % 2 : lo % 2 + hi - lo, :]
+            nc.vector.tensor_tensor(dev[:], sums, target_t[:, lo:hi, cols], ALU.subtract)
+            res = work.tile([P, hi - lo, HALF], F32, name="res", bufs=len(pieces))
+            nc.scalar.activation(out=res[:], in_=dev[:], func=ACT.Square)
+            nc.sync.dma_start(out=out_rows[:, lo:hi, cols], in_=res[:])

@@ -2,8 +2,8 @@ from contextlib import ExitStack
 
 import concourse.mybir as mybir
 
-T, S, NP, K, H, N = 2048, 1024, 512, 1024, 1536, 512
-FLOPS = 2 * K * H * S + 2 * H * N * NP
+T, S, PAIRS, K, H, N = 2048, 1024, 512, 1024, 1536, 512
+FLOPS = 2 * K * H * S + 2 * H * N * PAIRS
 
 F32 = mybir.dt.float32
 BF16 = mybir.dt.bfloat16
@@ -19,10 +19,17 @@ ACT = mybir.ActivationFunctionType
 P = 128
 PACK = 4
 PASS = P * PACK
-KP = K // PASS
-HP = H // PASS
+K_PASSES = K // PASS
+R_PASSES = H // PASS
 BANK = 512
-HALF = NP // 2
+HALF = PAIRS // 2
+GROUP = 16
+QUADRANT = 32
+RUN_BLOCKS = 2
+LINE = 4
+STAGING = 4
+WINDOWS = 3
+X_BANKS = 4
 
 
 def tile_list_shot_deviation_scores_kernel(
@@ -32,13 +39,13 @@ def tile_list_shot_deviation_scores_kernel(
     with ExitStack() as ctx:
         lists = ctx.enter_context(tc.tile_pool(name="lists", bufs=1))
         keep = ctx.enter_context(tc.tile_pool(name="keep", bufs=1))
-        stage = ctx.enter_context(tc.tile_pool(name="stage", bufs=4))
+        stage = ctx.enter_context(tc.tile_pool(name="stage", bufs=STAGING))
         work = ctx.enter_context(tc.tile_pool(name="work", bufs=2))
         psum = ctx.enter_context(tc.psum_pool(name="psum", bufs=1))
 
-        offs_t = lists.tile([P, S // 16], U16, name="offs_t")
-        pos1_t = lists.tile([P, NP // 16], U16, name="pos1_t")
-        pos2_t = lists.tile([P, NP // 16], U16, name="pos2_t")
+        offs_t = lists.tile([P, S // GROUP], U16, name="offs_t")
+        pos1_t = lists.tile([P, PAIRS // GROUP], U16, name="pos1_t")
+        pos2_t = lists.tile([P, PAIRS // GROUP], U16, name="pos2_t")
 
         scale_win = keep.tile([P, T], U8, name="scale_win", align_bytes=64)
         nc.gpsimd.memset(scale_win[:].bitcast(I32), 0)
@@ -55,58 +62,58 @@ def tile_list_shot_deviation_scores_kernel(
                 in_=tab_words[a].rearrange("p t i -> p (t i)").bitcast(I32),
             )
 
-        raw = {}
+        w1_raw = {}
 
         def load_w1(b, a):
-            raw[b, a] = staged([P, PACK, PASS], F32, f"raw{b}{a}")
+            w1_raw[b, a] = staged([P, PACK, PASS], F32, f"raw{b}{a}")
             rows = w1[a * PASS : (a + 1) * PASS, b * PASS : (b + 1) * PASS]
-            nc.sync.dma_start(out=raw[b, a][:], in_=rows.rearrange("(p j) c -> p j c", j=PACK))
+            nc.sync.dma_start(out=w1_raw[b, a][:], in_=rows.rearrange("(p i) c -> p i c", i=PACK))
 
         nc.sync.dma_start(offs_t[:], offs)
         load_w1(0, 0)
-        for a in range(KP):
-            for e in range(2):
+        for a in range(K_PASSES):
+            for e in range(RUN_BLOCKS):
                 nc.sync.dma_start(
-                    out=scale_win[4 * a + e : P : 16, :].bitcast(I32),
-                    in_=tab_scales[a, e:16:2, :].bitcast(I32),
+                    out=scale_win[PACK * a + e : P : GROUP, :].bitcast(I32),
+                    in_=tab_scales[a, e : P // 8 : RUN_BLOCKS, :].bitcast(I32),
                 )
         load_words(0)
         load_w1(0, 1)
         load_words(1)
         nc.sync.dma_start(pos1_t[:], pos1)
         nc.sync.dma_start(pos2_t[:], pos2)
-        gain_t = keep.tile([P, HP, PACK], F32, name="gain_t")
+        gain_t = keep.tile([P, R_PASSES, PACK], F32, name="gain_t")
         nc.gpsimd.dma_start(out=gain_t[:], in_=gain.rearrange("(b p t) -> p b t", p=P, t=PACK))
 
         scale_pick = keep.tile([P, S], U8, name="scale_pick", align_bytes=64)
         nc.vector.tensor_copy(scale_pick[:], scale_win[:].indirect(offs_t[:]))
         tab_plane = keep.tile([P, S], U8, name="tab_plane", align_bytes=64)
         nc.vector.tensor_copy(tab_plane[:].bitcast(I32), scale_pick[:].bitcast(I32))
-        for a in range(KP):
-            for e in range(2):
+        for a in range(K_PASSES):
+            for e in range(RUN_BLOCKS):
                 nc.sync.dma_start(
-                    out=tab_plane[4 * a + 2 + e : P : 32, :].bitcast(I32),
-                    in_=scale_pick[16 + 4 * a + e : P : 32, :].bitcast(I32),
+                    out=tab_plane[PACK * a + RUN_BLOCKS + e : P : QUADRANT, :].bitcast(I32),
+                    in_=scale_pick[GROUP + PACK * a + e : P : QUADRANT, :].bitcast(I32),
                 )
 
         word_pick = {}
 
         def gather_words(a):
             for c in range(S // BANK):
-                tile = keep.tile([P, BANK], U32, name=f"word_pick{a}{c}", align_bytes=64)
-                cols = slice(c * BANK // 16, (c + 1) * BANK // 16)
-                nc.vector.tensor_copy(tile[:], word_win[a][:].indirect(offs_t[:, cols]))
-                word_pick[a, c] = tile
+                word_pick[a, c] = keep.tile([P, BANK], U32, name=f"word_pick{a}{c}", align_bytes=64)
+                entries = slice(c * BANK // GROUP, (c + 1) * BANK // GROUP)
+                nc.vector.tensor_copy(word_pick[a, c][:], word_win[a][:].indirect(offs_t[:, entries]))
 
-        grouped = {}
+        w1_grouped = {}
         w1_codes = {}
         w1_plane = {}
 
         def round_w1(b, a, copy):
-            grouped[b, a] = work.tile([P, PACK, P, PACK], BF16, name="w1_grouped", align_bytes=64)
-            dst = grouped[b, a][:].rearrange("p t m j -> p m j t")
-            src = raw[b, a][:].rearrange("p j (m t) -> p m j t", t=PACK)
-            copy(dst, src)
+            w1_grouped[b, a] = work.tile([P, PACK, P, PACK], BF16, name="w1_grouped", align_bytes=64)
+            copy(
+                w1_grouped[b, a][:].rearrange("p t q i -> p q i t"),
+                w1_raw[b, a][:].rearrange("p i (q t) -> p q i t", t=PACK),
+            )
 
         def quantise_w1(b, a):
             w1_codes[b, a] = keep.tile([P, PASS], U32, name=f"w1_codes{b}{a}", align_bytes=64)
@@ -114,15 +121,15 @@ def tile_list_shot_deviation_scores_kernel(
             nc.vector.quantize_mx(
                 out=w1_codes[b, a][:].bitcast(FP8X4),
                 scales=w1_plane[b, a][:],
-                in_=grouped[b, a][:].rearrange("p t m j -> p (t m j)"),
+                in_=w1_grouped[b, a][:].rearrange("p t q i -> p (t q i)"),
             )
 
-        for a in range(KP):
+        for a in range(K_PASSES):
             round_w1(0, a, nc.scalar.copy)
             gather_words(a)
             quantise_w1(0, a)
-        for b in range(1, HP):
-            for a in range(KP):
+        for b in range(1, R_PASSES):
+            for a in range(K_PASSES):
                 load_w1(b, a)
 
         acc = {(h, u): psum.tile([P, 2, HALF], F32, name=f"acc{h}{u}") for h in range(2) for u in range(2)}
@@ -130,40 +137,52 @@ def tile_list_shot_deviation_scores_kernel(
         def closeness(b, t):
             banks = []
             for c in range(S // BANK):
-                bank = psum.tile([P, BANK], F32, name="x_bank", bufs=4)
-                for a in range(KP):
+                bank = psum.tile([P, BANK], F32, name="x_bank", bufs=X_BANKS)
+                for a in range(K_PASSES):
                     nc.tensor.matmul_mx(
                         out=bank[:],
                         lhsT=w1_codes[b, a][:, t * P : (t + 1) * P].bitcast(FP8X4),
                         lhsT_scale=w1_plane[b, a][:, t * P : (t + 1) * P],
                         rhs=word_pick[a, c][:].bitcast(FP8X4),
-                        rhs_scale=tab_plane[4 * a : P, c * BANK : (c + 1) * BANK],
+                        rhs_scale=tab_plane[PACK * a : P, c * BANK : (c + 1) * BANK],
                         start=(a == 0),
-                        stop=(a == KP - 1),
+                        stop=(a == K_PASSES - 1),
                     )
                 banks.append(bank)
             mag = work.tile([P, S], F32, name="mag")
             root = work.tile([P, S], F32, name="root")
-            close = work.tile([P, S], F32, name="close", bufs=3)
-            halves = [slice(c * BANK, (c + 1) * BANK) for c in range(S // BANK)]
-            for c, cols in enumerate(halves):
-                nc.scalar.activation(out=mag[:, cols], in_=banks[c][:], func=ACT.Abs)
-            for cols in halves:
-                nc.scalar.activation(out=root[:, cols], in_=mag[:, cols], func=ACT.Abs_reciprocal_sqrt, bias=1.0)
-            for cols in halves:
+            close = work.tile([P, S], F32, name="close", bufs=WINDOWS)
+            bank_cols = [slice(c * BANK, (c + 1) * BANK) for c in range(S // BANK)]
+            if (b, t) == (0, 0):
+                both = work.tile([P, 2, BANK], F32, name="both", bufs=1)
+                for side, sign in enumerate((1.0, -1.0)):
+                    nc.scalar.activation(
+                        out=both[:, side, :], in_=banks[0][:], func=ACT.Abs_reciprocal_sqrt, bias=1.0, scale=sign
+                    )
+                nc.vector.tensor_tensor(root[:, bank_cols[0]], both[:, 0, :], both[:, 1, :], ALU.min)
+                nc.scalar.activation(out=mag[:, bank_cols[1]], in_=banks[1][:], func=ACT.Abs)
+                nc.scalar.activation(
+                    out=root[:, bank_cols[1]], in_=mag[:, bank_cols[1]], func=ACT.Abs_reciprocal_sqrt, bias=1.0
+                )
+            else:
+                for bank, cols in zip(banks, bank_cols):
+                    nc.scalar.activation(out=mag[:, cols], in_=bank[:], func=ACT.Abs)
+                for cols in bank_cols:
+                    nc.scalar.activation(out=root[:, cols], in_=mag[:, cols], func=ACT.Abs_reciprocal_sqrt, bias=1.0)
+            for cols in bank_cols:
                 nc.scalar.activation(out=close[:, cols], in_=root[:, cols], func=ACT.Square)
             return close
 
         pair_halves = [slice(h * HALF, (h + 1) * HALF) for h in range(2)]
 
         def pair_up(b, t, close, first_h, larger):
-            first = work.tile([P, NP], F32, name="first")
-            second = work.tile([P, NP], F32, name="second")
+            first = work.tile([P, PAIRS], F32, name="first")
+            second = work.tile([P, PAIRS], F32, name="second")
             row_gain = gain_t[:, b, t : t + 1]
             nc.vector.tensor_copy(first[:], close[:].indirect(pos1_t[:]))
             nc.gpsimd.tensor_scalar(first_h[:, t, :], first[:], row_gain, 0.0, ALU.mult, ALU.add)
             for cols in pair_halves:
-                entries = slice(cols.start // 16, cols.stop // 16)
+                entries = slice(cols.start // GROUP, cols.stop // GROUP)
                 nc.vector.tensor_copy(second[:, cols], close[:].indirect(pos2_t[:, entries]))
             for cols in pair_halves:
                 nc.vector.scalar_tensor_tensor(
@@ -171,28 +190,28 @@ def tile_list_shot_deviation_scores_kernel(
                 )
 
         def multiply_w4(b, h, codes, plane):
-            for i in range(N // P):
+            for tile_n in range(N // P):
                 nc.tensor.matmul_mx(
-                    out=acc[h, i // 2][:, i % 2, :],
-                    lhsT=w4_codes[:, b, 2 * i * P : 2 * (i + 1) * P].bitcast(FP4X4),
-                    lhsT_scale=w4_plane[:, b, i * P : (i + 1) * P],
+                    out=acc[h, tile_n // 2][:, tile_n % 2, :],
+                    lhsT=w4_codes[:, b, 2 * tile_n * P : 2 * (tile_n + 1) * P].bitcast(FP4X4),
+                    lhsT_scale=w4_plane[:, b, tile_n * P : (tile_n + 1) * P],
                     rhs=codes.bitcast(FP8X4),
                     rhs_scale=plane,
-                    start=(b == 0 and i % 2 == 0),
-                    stop=(b == HP - 1 and i % 2 == 1),
+                    start=(b == 0 and tile_n % 2 == 0),
+                    stop=(b == R_PASSES - 1 and tile_n % 2 == 1),
                 )
 
         def second_stage(b, first_h, larger):
             z_grouped = []
             for cols in pair_halves:
-                tile = work.tile([P, HALF, PACK], BF16, name="z_grouped", align_bytes=64)
+                half = work.tile([P, HALF, PACK], BF16, name="z_grouped", align_bytes=64)
                 nc.vector.tensor_tensor(
-                    tile[:].rearrange("p (c i) t -> p c t i", i=4),
-                    larger[:, :, cols].rearrange("p t (c i) -> p c t i", i=4),
-                    first_h[:, :, cols].rearrange("p t (c i) -> p c t i", i=4),
+                    half[:].rearrange("p (run m) t -> p run t m", m=LINE),
+                    larger[:, :, cols].rearrange("p t (run m) -> p run t m", m=LINE),
+                    first_h[:, :, cols].rearrange("p t (run m) -> p run t m", m=LINE),
                     ALU.add,
                 )
-                z_grouped.append(tile)
+                z_grouped.append(half)
             for h in range(2):
                 z_codes = work.tile([P, HALF], U32, name="z_codes", align_bytes=64)
                 z_plane = work.tile([P, HALF], U8, name="z_plane", align_bytes=64)
@@ -203,45 +222,45 @@ def tile_list_shot_deviation_scores_kernel(
                 )
                 multiply_w4(b, h, z_codes[:], z_plane[:])
 
-        for a in range(KP):
+        close = closeness(0, 0)
+        for a in range(K_PASSES):
             round_w1(1, a, nc.vector.tensor_copy)
             quantise_w1(1, a)
-        round_w1(2, 0, nc.vector.tensor_copy)
-        quantise_w1(2, 0)
 
-        w4_codes = staged([P, HP, 2 * N], U8, "w4_codes")
+        w4_codes = staged([P, R_PASSES, 2 * N], U8, "w4_codes")
         nc.sync.dma_start(
             out=w4_codes[:].bitcast(I32), in_=w4_words.rearrange("a p c -> p a c").bitcast(I32)
         )
-        w4_plane = staged([P, HP, N], U8, "w4_plane")
+        w4_plane = staged([P, R_PASSES, N], U8, "w4_plane")
         nc.gpsimd.memset(w4_plane[:].bitcast(I32), 0)
-        for q in range(4):
+        for d in range(P // QUADRANT):
             nc.sync.dma_start(
-                out=w4_plane[32 * q : 32 * q + 4].bitcast(I32),
-                in_=w4_scales[:, 4 * q : 4 * q + 4, :].rearrange("a q c -> q a c").bitcast(I32),
+                out=w4_plane[QUADRANT * d : QUADRANT * d + 4].bitcast(I32),
+                in_=w4_scales[:, 4 * d : 4 * d + 4, :].rearrange("a s c -> s a c").bitcast(I32),
             )
 
-        for b in range(HP):
-            first_h = work.tile([P, PACK, NP], F32, name="first_h")
-            larger = work.tile([P, PACK, NP], F32, name="larger")
+        for b in range(R_PASSES):
+            first_h = work.tile([P, PACK, PAIRS], F32, name="first_h")
+            larger = work.tile([P, PACK, PAIRS], F32, name="larger")
             for t in range(PACK):
-                close = closeness(b, t)
+                if (b, t) != (0, 0):
+                    close = closeness(b, t)
                 pair_up(b, t, close, first_h, larger)
-                if (b, t) == (1, 0):
-                    round_w1(2, 1, nc.scalar.copy)
-                    quantise_w1(2, 1)
+                if b == 1 and t < K_PASSES:
+                    round_w1(R_PASSES - 1, t, nc.scalar.copy)
+                    quantise_w1(R_PASSES - 1, t)
             second_stage(b, first_h, larger)
 
-        target_t = staged([P, N // P, NP], F32, "target_t")
+        target_t = staged([P, N // P, PAIRS], F32, "target_t")
         nc.sync.dma_start(out=target_t[:], in_=target.rearrange("(i p) m -> p i m", p=P))
 
         out_rows = out.rearrange("(i p) m -> p i m", p=P)
         pieces = [(0, 0, 2), (0, 2, 4), (1, 0, 2), (1, 2, 3), (1, 3, 4)]
         for h, lo, hi in pieces:
             cols = pair_halves[h]
-            dev = work.tile([P, hi - lo, HALF], F32, name="dev", bufs=len(pieces))
+            deviation = work.tile([P, hi - lo, HALF], F32, name="dev", bufs=len(pieces))
             sums = acc[h, lo // 2][:, lo % 2 : lo % 2 + hi - lo, :]
-            nc.vector.tensor_tensor(dev[:], sums, target_t[:, lo:hi, cols], ALU.subtract)
-            res = work.tile([P, hi - lo, HALF], F32, name="res", bufs=len(pieces))
-            nc.scalar.activation(out=res[:], in_=dev[:], func=ACT.Square)
-            nc.sync.dma_start(out=out_rows[:, lo:hi, cols], in_=res[:])
+            nc.vector.tensor_tensor(deviation[:], sums, target_t[:, lo:hi, cols], ALU.subtract)
+            squared = work.tile([P, hi - lo, HALF], F32, name="res", bufs=len(pieces))
+            nc.scalar.activation(out=squared[:], in_=deviation[:], func=ACT.Square)
+            nc.sync.dma_start(out=out_rows[:, lo:hi, cols], in_=squared[:])

from contextlib import ExitStack

import concourse.mybir as mybir

T, S, PAIRS, K, H, N = 2048, 1024, 512, 1024, 1536, 512
FLOPS = 2 * K * H * S + 2 * H * N * PAIRS

F32 = mybir.dt.float32
BF16 = mybir.dt.bfloat16
I32 = mybir.dt.int32
U32 = mybir.dt.uint32
U16 = mybir.dt.uint16
U8 = mybir.dt.uint8
FP8X4 = mybir.dt.float8_e4m3fn_x4
FP4X4 = mybir.dt.float4_e2m1fn_x4
ALU = mybir.AluOpType
ACT = mybir.ActivationFunctionType

P = 128
PACK = 4
PASS = P * PACK
K_PASSES = K // PASS
R_PASSES = H // PASS
BANK = 512
HALF = PAIRS // 2
GROUP = 16
QUADRANT = 32
RUN_BLOCKS = 2
LINE = 4
STAGING = 4
WINDOWS = 3
X_BANKS = 4


def tile_list_shot_deviation_scores_kernel(
    tc, tab_words, tab_scales, offs, w1, gain, pos1, pos2, w4_words, w4_scales, target, out
):
    nc = tc.nc
    with ExitStack() as ctx:
        lists = ctx.enter_context(tc.tile_pool(name="lists", bufs=1))
        keep = ctx.enter_context(tc.tile_pool(name="keep", bufs=1))
        stage = ctx.enter_context(tc.tile_pool(name="stage", bufs=STAGING))
        work = ctx.enter_context(tc.tile_pool(name="work", bufs=2))
        psum = ctx.enter_context(tc.psum_pool(name="psum", bufs=1))

        offs_t = lists.tile([P, S // GROUP], U16, name="offs_t")
        pos1_t = lists.tile([P, PAIRS // GROUP], U16, name="pos1_t")
        pos2_t = lists.tile([P, PAIRS // GROUP], U16, name="pos2_t")

        scale_win = keep.tile([P, T], U8, name="scale_win", align_bytes=64)
        nc.gpsimd.memset(scale_win[:].bitcast(I32), 0)

        def staged(shape, dtype, name):
            return stage.tile(shape, dtype, name=name, tag="staged", align_bytes=64)

        word_win = {}

        def load_words(a):
            word_win[a] = staged([P, T], U32, f"word_win{a}")
            nc.sync.dma_start(
                out=word_win[a][:].bitcast(I32),
                in_=tab_words[a].rearrange("p t i -> p (t i)").bitcast(I32),
            )

        w1_raw = {}

        def load_w1(b, a):
            w1_raw[b, a] = staged([P, PACK, PASS], F32, f"raw{b}{a}")
            rows = w1[a * PASS : (a + 1) * PASS, b * PASS : (b + 1) * PASS]
            nc.sync.dma_start(out=w1_raw[b, a][:], in_=rows.rearrange("(p i) c -> p i c", i=PACK))

        nc.sync.dma_start(offs_t[:], offs)
        load_w1(0, 0)
        for a in range(K_PASSES):
            for e in range(RUN_BLOCKS):
                nc.sync.dma_start(
                    out=scale_win[PACK * a + e : P : GROUP, :].bitcast(I32),
                    in_=tab_scales[a, e : P // 8 : RUN_BLOCKS, :].bitcast(I32),
                )
        load_words(0)
        load_w1(0, 1)
        load_words(1)
        nc.sync.dma_start(pos1_t[:], pos1)
        nc.sync.dma_start(pos2_t[:], pos2)
        gain_t = keep.tile([P, R_PASSES, PACK], F32, name="gain_t")
        nc.gpsimd.dma_start(out=gain_t[:], in_=gain.rearrange("(b p t) -> p b t", p=P, t=PACK))

        scale_pick = keep.tile([P, S], U8, name="scale_pick", align_bytes=64)
        nc.vector.tensor_copy(scale_pick[:], scale_win[:].indirect(offs_t[:]))
        tab_plane = keep.tile([P, S], U8, name="tab_plane", align_bytes=64)
        nc.vector.tensor_copy(tab_plane[:].bitcast(I32), scale_pick[:].bitcast(I32))
        for a in range(K_PASSES):
            for e in range(RUN_BLOCKS):
                nc.sync.dma_start(
                    out=tab_plane[PACK * a + RUN_BLOCKS + e : P : QUADRANT, :].bitcast(I32),
                    in_=scale_pick[GROUP + PACK * a + e : P : QUADRANT, :].bitcast(I32),
                )

        word_pick = {}

        def gather_words(a):
            for c in range(S // BANK):
                word_pick[a, c] = keep.tile([P, BANK], U32, name=f"word_pick{a}{c}", align_bytes=64)
                entries = slice(c * BANK // GROUP, (c + 1) * BANK // GROUP)
                nc.vector.tensor_copy(word_pick[a, c][:], word_win[a][:].indirect(offs_t[:, entries]))

        w1_grouped = {}
        w1_codes = {}
        w1_plane = {}

        def round_w1(b, a, copy):
            w1_grouped[b, a] = work.tile([P, PACK, P, PACK], BF16, name="w1_grouped", align_bytes=64)
            copy(
                w1_grouped[b, a][:].rearrange("p t q i -> p q i t"),
                w1_raw[b, a][:].rearrange("p i (q t) -> p q i t", t=PACK),
            )

        def quantise_w1(b, a):
            w1_codes[b, a] = keep.tile([P, PASS], U32, name=f"w1_codes{b}{a}", align_bytes=64)
            w1_plane[b, a] = keep.tile([P, PASS], U8, name=f"w1_plane{b}{a}", align_bytes=64)
            nc.vector.quantize_mx(
                out=w1_codes[b, a][:].bitcast(FP8X4),
                scales=w1_plane[b, a][:],
                in_=w1_grouped[b, a][:].rearrange("p t q i -> p (t q i)"),
            )

        for a in range(K_PASSES):
            round_w1(0, a, nc.scalar.copy)
            gather_words(a)
            quantise_w1(0, a)
        for b in range(1, R_PASSES):
            for a in range(K_PASSES):
                load_w1(b, a)

        acc = {(h, u): psum.tile([P, 2, HALF], F32, name=f"acc{h}{u}") for h in range(2) for u in range(2)}

        def closeness(b, t):
            banks = []
            for c in range(S // BANK):
                bank = psum.tile([P, BANK], F32, name="x_bank", bufs=X_BANKS)
                for a in range(K_PASSES):
                    nc.tensor.matmul_mx(
                        out=bank[:],
                        lhsT=w1_codes[b, a][:, t * P : (t + 1) * P].bitcast(FP8X4),
                        lhsT_scale=w1_plane[b, a][:, t * P : (t + 1) * P],
                        rhs=word_pick[a, c][:].bitcast(FP8X4),
                        rhs_scale=tab_plane[PACK * a : P, c * BANK : (c + 1) * BANK],
                        start=(a == 0),
                        stop=(a == K_PASSES - 1),
                    )
                banks.append(bank)
            mag = work.tile([P, S], F32, name="mag")
            root = work.tile([P, S], F32, name="root")
            close = work.tile([P, S], F32, name="close", bufs=WINDOWS)
            bank_cols = [slice(c * BANK, (c + 1) * BANK) for c in range(S // BANK)]
            if (b, t) == (0, 0):
                both = work.tile([P, 2, BANK], F32, name="both", bufs=1)
                for side, sign in enumerate((1.0, -1.0)):
                    nc.scalar.activation(
                        out=both[:, side, :], in_=banks[0][:], func=ACT.Abs_reciprocal_sqrt, bias=1.0, scale=sign
                    )
                nc.vector.tensor_tensor(root[:, bank_cols[0]], both[:, 0, :], both[:, 1, :], ALU.min)
                nc.scalar.activation(out=mag[:, bank_cols[1]], in_=banks[1][:], func=ACT.Abs)
                nc.scalar.activation(
                    out=root[:, bank_cols[1]], in_=mag[:, bank_cols[1]], func=ACT.Abs_reciprocal_sqrt, bias=1.0
                )
            else:
                for bank, cols in zip(banks, bank_cols):
                    nc.scalar.activation(out=mag[:, cols], in_=bank[:], func=ACT.Abs)
                for cols in bank_cols:
                    nc.scalar.activation(out=root[:, cols], in_=mag[:, cols], func=ACT.Abs_reciprocal_sqrt, bias=1.0)
            for cols in bank_cols:
                nc.scalar.activation(out=close[:, cols], in_=root[:, cols], func=ACT.Square)
            return close

        pair_halves = [slice(h * HALF, (h + 1) * HALF) for h in range(2)]

        def pair_up(b, t, close, first_h, larger):
            first = work.tile([P, PAIRS], F32, name="first")
            second = work.tile([P, PAIRS], F32, name="second")
            row_gain = gain_t[:, b, t : t + 1]
            nc.vector.tensor_copy(first[:], close[:].indirect(pos1_t[:]))
            nc.gpsimd.tensor_scalar(first_h[:, t, :], first[:], row_gain, 0.0, ALU.mult, ALU.add)
            for cols in pair_halves:
                entries = slice(cols.start // GROUP, cols.stop // GROUP)
                nc.vector.tensor_copy(second[:, cols], close[:].indirect(pos2_t[:, entries]))
            for cols in pair_halves:
                nc.vector.scalar_tensor_tensor(
                    larger[:, t, cols], second[:, cols], row_gain, first_h[:, t, cols], ALU.mult, ALU.max
                )

        def multiply_w4(b, h, codes, plane):
            for tile_n in range(N // P):
                nc.tensor.matmul_mx(
                    out=acc[h, tile_n // 2][:, tile_n % 2, :],
                    lhsT=w4_codes[:, b, 2 * tile_n * P : 2 * (tile_n + 1) * P].bitcast(FP4X4),
                    lhsT_scale=w4_plane[:, b, tile_n * P : (tile_n + 1) * P],
                    rhs=codes.bitcast(FP8X4),
                    rhs_scale=plane,
                    start=(b == 0 and tile_n % 2 == 0),
                    stop=(b == R_PASSES - 1 and tile_n % 2 == 1),
                )

        def second_stage(b, first_h, larger):
            z_grouped = []
            for cols in pair_halves:
                half = work.tile([P, HALF, PACK], BF16, name="z_grouped", align_bytes=64)
                nc.vector.tensor_tensor(
                    half[:].rearrange("p (run m) t -> p run t m", m=LINE),
                    larger[:, :, cols].rearrange("p t (run m) -> p run t m", m=LINE),
                    first_h[:, :, cols].rearrange("p t (run m) -> p run t m", m=LINE),
                    ALU.add,
                )
                z_grouped.append(half)
            for h in range(2):
                z_codes = work.tile([P, HALF], U32, name="z_codes", align_bytes=64)
                z_plane = work.tile([P, HALF], U8, name="z_plane", align_bytes=64)
                nc.vector.quantize_mx(
                    out=z_codes[:].bitcast(FP8X4),
                    scales=z_plane[:],
                    in_=z_grouped[h][:].rearrange("p m t -> p (m t)"),
                )
                multiply_w4(b, h, z_codes[:], z_plane[:])

        close = closeness(0, 0)
        for a in range(K_PASSES):
            round_w1(1, a, nc.vector.tensor_copy)
            quantise_w1(1, a)

        w4_codes = staged([P, R_PASSES, 2 * N], U8, "w4_codes")
        nc.sync.dma_start(
            out=w4_codes[:].bitcast(I32), in_=w4_words.rearrange("a p c -> p a c").bitcast(I32)
        )
        w4_plane = staged([P, R_PASSES, N], U8, "w4_plane")
        nc.gpsimd.memset(w4_plane[:].bitcast(I32), 0)
        for d in range(P // QUADRANT):
            nc.sync.dma_start(
                out=w4_plane[QUADRANT * d : QUADRANT * d + 4].bitcast(I32),
                in_=w4_scales[:, 4 * d : 4 * d + 4, :].rearrange("a s c -> s a c").bitcast(I32),
            )

        for b in range(R_PASSES):
            first_h = work.tile([P, PACK, PAIRS], F32, name="first_h")
            larger = work.tile([P, PACK, PAIRS], F32, name="larger")
            for t in range(PACK):
                if (b, t) != (0, 0):
                    close = closeness(b, t)
                pair_up(b, t, close, first_h, larger)
                if b == 1 and t < K_PASSES:
                    round_w1(R_PASSES - 1, t, nc.scalar.copy)
                    quantise_w1(R_PASSES - 1, t)
            second_stage(b, first_h, larger)

        target_t = staged([P, N // P, PAIRS], F32, "target_t")
        nc.sync.dma_start(out=target_t[:], in_=target.rearrange("(i p) m -> p i m", p=P))

        out_rows = out.rearrange("(i p) m -> p i m", p=P)
        pieces = [(0, 0, 2), (0, 2, 4), (1, 0, 2), (1, 2, 3), (1, 3, 4)]
        for h, lo, hi in pieces:
            cols = pair_halves[h]
            deviation = work.tile([P, hi - lo, HALF], F32, name="dev", bufs=len(pieces))
            sums = acc[h, lo // 2][:, lo % 2 : lo % 2 + hi - lo, :]
            nc.vector.tensor_tensor(deviation[:], sums, target_t[:, lo:hi, cols], ALU.subtract)
            squared = work.tile([P, hi - lo, HALF], F32, name="res", bufs=len(pieces))
            nc.scalar.activation(out=squared[:], in_=deviation[:], func=ACT.Square)
            nc.sync.dma_start(out=out_rows[:, lo:hi, cols], in_=squared[:])
